import numpy as np
import ml_dtypes


def mxq(x, axis, fmt="e4m3"):
    dtype, down = {"e4m3": (ml_dtypes.float8_e4m3fn, 7), "e5m2": (ml_dtypes.float8_e5m2, 14)}[fmt]
    v = np.moveaxis(np.asarray(x, np.float32).astype(ml_dtypes.bfloat16).astype(np.float64), axis, -1)
    blocks = v.reshape(v.shape[:-1] + (-1, 32))
    amax = np.abs(blocks).max(-1, keepdims=True)
    byte = np.maximum(np.where(amax > 0, np.frexp(amax)[1] - 1 + 127, 0) - down, 1)
    scale = np.exp2(byte - 127.0)
    codes = (blocks / scale).astype(np.float32).astype(dtype).astype(np.float64)
    return np.moveaxis((codes * scale).reshape(v.shape), -1, axis)


WIDE = False


def mx_kscale(k):
    if not WIDE:
        return np.ones(k)
    levels = np.array([10, -10, 5, -5, 0])
    if k % 512:
        return np.exp2(np.random.permutation(np.resize(levels, k // 32))).repeat(32)
    a = np.empty((k // 512, 16))
    for p in range(k // 512):
        a[p, :8] = np.random.permutation(np.resize(levels, 8))
        for g in range(8):
            far = levels[np.abs(levels - a[p, g]) >= 10]
            a[p, g + 8] = far[np.random.randint(len(far))]
    return np.exp2(a.ravel()).repeat(32)


def f64(x):
    return np.asarray(x).astype(np.float64)


def striped(idx):
    return np.tile(np.asarray(idx).reshape(-1, 16).T, (8, 1)).astype(np.uint16)


def unstriped(offs):
    return offs[:16].T.reshape(-1).astype(np.int64)


E2M1 = np.array([0.0, 0.5, 1.0, 1.5, 2.0, 3.0, 4.0, 6.0, -0.0, -0.5, -1.0, -1.5, -2.0, -3.0, -4.0, -6.0])


def pack_weight(w, fmt):
    k, n = w.shape
    w = f64(np.asarray(w, np.float32).astype(ml_dtypes.bfloat16)).reshape(k // 32, 32, n)
    amax = np.abs(w).max(1)
    if fmt == "e4m3":
        byte = np.frexp(amax)[1] - 1 + 127 - 7
    else:
        mant, ex = np.frexp(amax / 6.0)
        byte = np.where(mant > 0.5, ex, ex - 1) + 127
    byte = np.clip(np.where(amax > 0, byte, 1), 1, 254)
    scaled = (w * np.exp2(127.0 - byte)[:, None, :]).reshape(k, n).astype(np.float32)
    by_word = np.ascontiguousarray(scaled.reshape(k // 512, 128, 4, n).transpose(0, 1, 3, 2))
    if fmt == "e4m3":
        words = by_word.astype(ml_dtypes.float8_e4m3fn).view(np.uint8)
    else:
        c = by_word.astype(ml_dtypes.float4_e2m1fn).view(np.uint8) & 0xF
        words = (c[..., 0::2] | (c[..., 1::2] << 4)).reshape(k // 512, 128, 2 * n)
    return np.ascontiguousarray(words), np.ascontiguousarray(byte.astype(np.uint8).reshape(k // 512, 16, n))


def unpack_weight(words, scales, fmt):
    g, _, n = scales.shape
    words = np.ascontiguousarray(words).reshape(g, 128, n, -1)
    if fmt == "e4m3":
        vals = words.view(ml_dtypes.float8_e4m3fn).astype(np.float64)
    else:
        nib = np.empty((g, 128, n, 4), np.uint8)
        nib[..., 0::2] = words & 0xF
        nib[..., 1::2] = words >> 4
        vals = E2M1[nib]
    vals = vals * np.repeat(np.exp2(scales.astype(np.float64) - 127.0), 8, axis=1)[..., None]
    return vals.transpose(0, 1, 3, 2).reshape(g * 512, n)


def sigmoid(v):
    return 1.0 / (1.0 + np.exp(-v))


def sgn(shape):
    return np.random.uniform(0.5, 2.0, shape) * np.where(np.random.standard_normal(shape) < 0, -1.0, 1.0)


K, T, J, R, F, Z, O, Q, N, E = 512, 1024, 256, 512, 512, 1024, 128, 128, 256, 256


def setup_inputs():
    n = np.random.standard_normal
    idx = np.random.permutation(T)[:J]
    idx2 = np.random.permutation(Z)[:J]
    idx3 = np.random.permutation(J)[:O]
    idx4 = np.random.permutation(J)[:O]
    idx5 = np.random.permutation(J)[:O]
    idx6 = np.random.permutation(J)[:O]
    idx7 = np.random.permutation(E)[:O]
    fk = mx_kscale(K)
    ff = mx_kscale(F)
    fr = mx_kscale(R)
    fr = fr / fr.max()
    xtp = pack_weight(n((K, T)) / fk[:, None], "e2m1")
    xop = pack_weight(n((F, Z)) / ff[:, None], "e4m3")
    wp = pack_weight(n((K, R)) * 1 / np.sqrt(K) * fk[:, None], "e4m3")
    w0p = pack_weight(n((F, R)) * 1 / np.sqrt(F) * ff[:, None], "e4m3")
    wbp = pack_weight(n((R, N)) * 1 / np.sqrt(R) / fr[:, None], "e4m3")
    return {
        "xt_words": xtp[0],
        "xt_scales": xtp[1],
        "xo_words": xop[0],
        "xo_scales": xop[1],
        "w_words": wp[0],
        "w_scales": wp[1],
        "w0_words": w0p[0],
        "w0_scales": w0p[1],
        "sa": (np.random.uniform(0.5, 1.6, (Q, 1)) * fr[::4, None]).astype(np.float32),
        "sb": (sgn((Q, 1)) * fr[::4, None]).astype(np.float32),
        "sd": (0.2 * sgn((Q, 1))).astype(np.float32),
        "bd": (np.random.uniform(-0.5, 0.3, (Q, 1)) + np.log(fr[::4])[:, None]).astype(np.float32),
        "se": (0.4 * sgn((Q, 1))).astype(np.float32),
        "be": (np.random.uniform(-2.2, 0.2, (Q, 1)) + np.log(fr[::4])[:, None]).astype(np.float32),
        "wb_words": wbp[0],
        "wb_scales": wbp[1],
        "so": (np.random.uniform(0.5, 1.6, (N, 1))).astype(np.float32),
        "offs": striped(idx),
        "offs2": striped(idx2),
        "offs3": striped(idx3),
        "offs4": striped(idx4),
        "offs5": striped(idx5),
        "offs6": striped(idx6),
        "offs7": striped(idx7),
    }


def reference(xt_words, xt_scales, xo_words, xo_scales, w_words, w_scales, w0_words, w0_scales, sa, sb, sd, bd, se, be, wb_words, wb_scales, so, offs, offs2, offs3, offs4, offs5, offs6, offs7):
    idx = unstriped(offs)
    idx2 = unstriped(offs2)
    idx3 = unstriped(offs3)
    idx4 = unstriped(offs4)
    idx5 = unstriped(offs5)
    idx6 = unstriped(offs6)
    idx7 = unstriped(offs7)
    xtu = unpack_weight(xt_words, xt_scales, "e2m1")
    xou = unpack_weight(xo_words, xo_scales, "e4m3")
    wu = unpack_weight(w_words, w_scales, "e4m3")
    w0u = unpack_weight(w0_words, w0_scales, "e4m3")
    wbu = unpack_weight(wb_words, wb_scales, "e4m3")
    xtidxg = xtu[:, idx]
    xoidx2g = xou[:, idx2]
    a = wu.T @ xtidxg + w0u.T @ xoidx2g
    a0 = a[0::4]
    a1 = a[1::4]
    a2 = a[2::4]
    a3 = a[3::4]
    v0 = a0[:, idx3] * f64(sa)
    v1 = a1[:, idx4] * f64(sb)
    v2 = np.exp(a2[:, idx5] * f64(sd) + f64(bd))
    v3 = sigmoid(a3[:, idx6] * f64(se) + f64(be))
    hid = np.stack([v0, v1, v2, v3], axis=1).reshape(R, O)
    hidq = mxq(hid, 0, "e4m3")
    p = wbu.T @ hidq
    y = np.zeros((N, E))
    y[:, idx7] = p * f64(so)
    return y

@@ -1,0 +1,159 @@
+from contextlib import ExitStack
+
+import concourse.mybir as mybir
+
+K, T, J, R, O, N, E = 512, 1024, 256, 512, 128, 256, 256
+FLOPS = 2 * (2 * K * R * J + R * N * O)
+
+F32 = mybir.dt.float32
+BF16 = mybir.dt.bfloat16
+I32 = mybir.dt.int32
+U32 = mybir.dt.uint32
+U16 = mybir.dt.uint16
+U8 = mybir.dt.uint8
+FP8X4 = mybir.dt.float8_e4m3fn_x4
+FP4X4 = mybir.dt.float4_e2m1fn_x4
+ACT = mybir.ActivationFunctionType
+
+P = 128
+HALF = O // 2
+
+
+def tile_list_quarterlaws_kernel(tc, xt_words, xt_scales, xo_words, xo_scales, w_words, w_scales,
+                                      w0_words, w0_scales, sa, sb, sd, bd, se, be, wb_words, wb_scales, so,
+                                      offs, offs2, offs3, offs4, offs5, offs6, offs7, out):
+    nc = tc.nc
+    with ExitStack() as ctx:
+        keep = ctx.enter_context(tc.tile_pool(name="keep", bufs=1))
+        psum = ctx.enter_context(tc.psum_pool(name="psum", bufs=1))
+
+        def sb_tile(name, shape, dtype):
+            return keep.tile(shape, dtype, name=name, align_bytes=64)
+
+        def words_view(words):
+            return words[0].rearrange("p n t -> p (n t)").bitcast(I32)
+
+        def by_residue(scales):
+            return scales[0].bitcast(I32).rearrange("(q r) c -> r q c", r=4)
+
+        tok_list = sb_tile("tok_list", [P, J // 16], U16)
+        note_list = sb_tile("note_list", [P, J // 16], U16)
+        law_lists = [sb_tile("law_list%d" % g, [P, O // 16], U16) for g in range(4)]
+        put_list = sb_tile("put_list", [P, O // 16], U16)
+
+        xt_w = sb_tile("xt_w", [P, T], U16)
+        xt_s = sb_tile("xt_s", [P, T], U8)
+        xo_w = sb_tile("xo_w", [P, T], U32)
+        xo_s = sb_tile("xo_s", [P, T], U8)
+        w_w = sb_tile("w_w", [P, R], U32)
+        w0_w = sb_tile("w0_w", [P, R], U32)
+        wb_w = sb_tile("wb_w", [P, N], U32)
+        ws_stage = sb_tile("ws_stage", [32, 4, R // 4], I32)
+        wbs_stage = sb_tile("wbs_stage", [4, 4, N // 4], I32)
+        ws_spread = sb_tile("ws_spread", [P, R], U8)
+        ws_dealt = sb_tile("ws_dealt", [P, R], U8)
+        wb_s = sb_tile("wb_s", [P, N], U8)
+        pages = [sb_tile("page%d" % t, [P, E], F32) for t in range(2)]
+        sa_t, sb_t, sd_t, bd_t, se_t, be_t = [sb_tile(n, [P, 1], F32) for n in ("sa_t", "sb_t", "sd_t", "bd_t", "se_t", "be_t")]
+        so_t = sb_tile("so_t", [P, 2], F32)
+
+        nc.gpsimd.memset(xt_s[:].bitcast(I32), 0)
+        nc.gpsimd.memset(ws_stage[:], 0)
+        nc.vector.memset(xo_s[:].bitcast(I32), 0)
+
+        nc.sync.dma_start(tok_list[:], offs)
+        nc.sync.dma_start(note_list[:], offs2)
+        for q in range(4):
+            nc.scalar.dma_start(xt_s[32 * q : 32 * q + 4, :].bitcast(I32), xt_scales[0, 4 * q : 4 * q + 4, :].bitcast(I32))
+        nc.sync.dma_start(xt_w[:].bitcast(I32), xt_words[0].bitcast(I32))
+        nc.sync.dma_start(w_w[:].bitcast(I32), words_view(w_words))
+        nc.sync.dma_start(xo_w[:].bitcast(I32), words_view(xo_words))
+        nc.sync.dma_start(w0_w[:].bitcast(I32), words_view(w0_words))
+        for q in range(4):
+            nc.scalar.dma_start(xo_s[32 * q : 32 * q + 4, :].bitcast(I32), xo_scales[0, 4 * q : 4 * q + 4, :].bitcast(I32))
+        nc.gpsimd.dma_start(ws_stage[0:4, :, :], by_residue(w_scales))
+        nc.gpsimd.dma_start(ws_stage[4:8, :, :], by_residue(w0_scales))
+        nc.sync.dma_start(law_lists[2][:], offs5)
+        nc.sync.dma_start(sd_t[:], sd)
+        nc.sync.dma_start(bd_t[:], bd)
+        nc.sync.dma_start(law_lists[3][:], offs6)
+        nc.sync.dma_start(se_t[:], se)
+        nc.sync.dma_start(be_t[:], be)
+        nc.sync.dma_start(law_lists[0][:], offs3)
+        nc.sync.dma_start(sa_t[:], sa)
+        nc.sync.dma_start(law_lists[1][:], offs4)
+        nc.sync.dma_start(sb_t[:], sb)
+        nc.sync.dma_start(wb_w[:].bitcast(I32), words_view(wb_words))
+        nc.sync.dma_start(wbs_stage[:], by_residue(wb_scales))
+        nc.sync.dma_start(put_list[:], offs7)
+        with nc.allow_non_contiguous_dma(reason="one float32 a partition and output tile"):
+            nc.sync.dma_start(so_t[:], so.rearrange("(t p) o -> p (t o)", p=P))
+
+        nc.vector.memset(wb_s[:].bitcast(I32), 0)
+        for t in range(2):
+            nc.vector.memset(pages[t][:], 0.0)
+
+        xt_gs = sb_tile("xt_gs", [P, J], U8)
+        xt_gw = sb_tile("xt_gw", [P, J], U16)
+        xo_gs = sb_tile("xo_gs", [P, J], U8)
+        xo_gw = sb_tile("xo_gw", [P, J], U32)
+        nc.vector.tensor_copy(xt_gs[:], xt_s[:].indirect(tok_list[:]))
+        nc.vector.tensor_copy(xt_gw[:], xt_w[:].indirect(tok_list[:]))
+
+        for q in range(4):
+            nc.vector.tensor_copy(ws_spread[32 * q : 32 * q + 32, :].bitcast(I32), ws_stage[:, q, :])
+        nc.vector.tensor_copy(ws_dealt[:].rearrange("p (g q) -> p q g", g=4), ws_spread[:].rearrange("p (q g) -> p q g", g=4))
+
+        nc.vector.tensor_copy(xo_gs[:], xo_s[:].indirect(note_list[:]))
+        nc.vector.tensor_copy(xo_gw[:], xo_w[:].indirect(note_list[:]))
+
+        w_d = sb_tile("w_d", [P, R], U32)
+        nc.scalar.copy(w_d[:].rearrange("p (g q) -> p q g", g=4), w_w[:].rearrange("p (q g) -> p q g", g=4))
+        w0_d = sb_tile("w0_d", [P, R], U32)
+        w0_in = w0_w[:].rearrange("p (q g) -> p q g", g=4)
+        w0_out = w0_d[:].rearrange("p (g q) -> p q g", g=4)
+        for g0, g1 in ((2, 3), (3, 4), (0, 2)):
+            nc.scalar.copy(w0_out[:, :, g0:g1], w0_in[:, :, g0:g1])
+
+        order = (2, 3, 0, 1)
+        acc = {g: psum.tile([P, J], F32, name="acc%d" % g) for g in order}
+        for g in order:
+            cols = slice(g * P, (g + 1) * P)
+            nc.tensor.matmul_mx(out=acc[g][:], lhsT=w_d[:, cols].bitcast(FP8X4), lhsT_scale=ws_dealt[:, cols],
+                                rhs=xt_gw[:].bitcast(FP4X4), rhs_scale=xt_gs[:], start=True, stop=False)
+        a = {}
+        for g in order:
+            cols = slice(g * P, (g + 1) * P)
+            nc.tensor.matmul_mx(out=acc[g][:], lhsT=w0_d[:, cols].bitcast(FP8X4), lhsT_scale=ws_dealt[4:P, cols],
+                                rhs=xo_gw[:].bitcast(FP8X4), rhs_scale=xo_gs[:], start=False, stop=True)
+            a[g] = sb_tile("a%d" % g, [P, J], F32)
+            nc.vector.tensor_copy(a[g][:], acc[g][:])
+
+        for q in range(4):
+            nc.vector.tensor_copy(wb_s[32 * q : 32 * q + 4, :].bitcast(I32), wbs_stage[:, q, :])
+
+        hid = sb_tile("hid", [P, 4 * O], BF16)
+        nc.scalar.activation(hid[:, 2 : 4 * O : 4], a[2][:].indirect(law_lists[2][:]), ACT.Exp, bias=bd_t[:], scale=sd_t[:])
+        p_sb = {}
+        for h in range(2):
+            c0, c1 = 4 * HALF * h, 4 * HALF * (h + 1)
+            ls = slice(h * HALF // 16, (h + 1) * HALF // 16)
+            nc.scalar.activation(hid[:, c0 + 3 : c1 : 4], a[3][:].indirect(law_lists[3][:, ls]), ACT.Sigmoid, bias=be_t[:], scale=se_t[:])
+            nc.scalar.activation(hid[:, c0 : c1 : 4], a[0][:].indirect(law_lists[0][:, ls]), ACT.Copy, scale=sa_t[:])
+            nc.scalar.activation(hid[:, c0 + 1 : c1 : 4], a[1][:].indirect(law_lists[1][:, ls]), ACT.Copy, scale=sb_t[:])
+            codes = sb_tile("codes%d" % h, [P, HALF], U32)
+            scales = sb_tile("scales%d" % h, [P, HALF], U8)
+            nc.vector.quantize_mx(out=codes[:].bitcast(FP8X4), scales=scales[:], in_=hid[:, c0:c1])
+            for t in range(2):
+                cols = slice(t * P, (t + 1) * P)
+                p_ps = psum.tile([P, HALF], F32, name="p_ps%d%d" % (h, t))
+                nc.tensor.matmul_mx(out=p_ps[:], lhsT=wb_w[:, cols].bitcast(FP8X4), lhsT_scale=wb_s[:, cols],
+                                    rhs=codes[:].bitcast(FP8X4), rhs_scale=scales[:], start=True, stop=True)
+                p_sb[h, t] = sb_tile("p_sb%d%d" % (h, t), [P, HALF], F32)
+                nc.vector.tensor_copy(p_sb[h, t][:], p_ps[:])
+        for h in range(2):
+            ls = slice(h * HALF // 16, (h + 1) * HALF // 16)
+            for t in range(2):
+                nc.scalar.activation(pages[t][:].indirect(put_list[:, ls]), p_sb[h, t][:], ACT.Copy, scale=so_t[:, t : t + 1])
+        for t in range(2):
+            nc.sync.dma_start(out[t * P : (t + 1) * P, :], pages[t][:])

@@ -36,6 +36,10 @@ def tile_list_quarterlaws_kernel(tc, xt_words, xt_scales, xo_words, xo_scales, w
         def by_residue(scales):
             return scales[0].bitcast(I32).rearrange("(q r) c -> r q c", r=4)
 
+        def spread(rows, live, width):
+            nc.vector.tensor_copy(rows[32 : 32 + live, 0 : 3 * width], rows[0:live, width : 4 * width])
+            nc.vector.tensor_copy(rows[64:128, 0:width], rows[0:64, 2 * width : 3 * width])
+
         tok_list = sb_tile("tok_list", [P, J // 16], U16)
         note_list = sb_tile("note_list", [P, J // 16], U16)
         law_lists = [sb_tile("law_list%d" % g, [P, O // 16], U16) for g in range(4)]
@@ -48,48 +52,52 @@ def tile_list_quarterlaws_kernel(tc, xt_words, xt_scales, xo_words, xo_scales, w
         w_w = sb_tile("w_w", [P, R], U32)
         w0_w = sb_tile("w0_w", [P, R], U32)
         wb_w = sb_tile("wb_w", [P, N], U32)
-        ws_stage = sb_tile("ws_stage", [32, 4, R // 4], I32)
-        wbs_stage = sb_tile("wbs_stage", [4, 4, N // 4], I32)
-        ws_spread = sb_tile("ws_spread", [P, R], U8)
+        ws_rows = sb_tile("ws_rows", [P, R], I32)
+        wbs_rows = sb_tile("wbs_rows", [P, N], I32)
+        ws_stage = sb_tile("ws_stage", [8, R], I32)
         ws_dealt = sb_tile("ws_dealt", [P, R], U8)
-        wb_s = sb_tile("wb_s", [P, N], U8)
         pages = [sb_tile("page%d" % t, [P, E], F32) for t in range(2)]
         sa_t, sb_t, sd_t, bd_t, se_t, be_t = [sb_tile(n, [P, 1], F32) for n in ("sa_t", "sb_t", "sd_t", "bd_t", "se_t", "be_t")]
         so_t = sb_tile("so_t", [P, 2], F32)
 
-        nc.gpsimd.memset(xt_s[:].bitcast(I32), 0)
-        nc.gpsimd.memset(ws_stage[:], 0)
+        def clear_even_blocks(engine, rows):
+            engine.memset(rows[0:64, :].rearrange("p (h l c) -> p h l c", h=2, l=2)[:, :, 0, :], 0)
+
         nc.vector.memset(xo_s[:].bitcast(I32), 0)
+        nc.vector.memset(xt_s[:].bitcast(I32), 0)
+        clear_even_blocks(nc.vector, ws_rows)
+        clear_even_blocks(nc.vector, wbs_rows)
+
+        def scale_rows(queue, plane, scales, q):
+            queue.dma_start(plane[32 * q : 32 * q + 4, :].bitcast(I32), scales[0, 4 * q : 4 * q + 4, :].bitcast(I32))
 
         nc.sync.dma_start(tok_list[:], offs)
+        nc.scalar.dma_start(ws_stage[0:4, :].rearrange("r (q c) -> r q c", q=4), by_residue(w_scales))
         nc.sync.dma_start(note_list[:], offs2)
-        for q in range(4):
-            nc.scalar.dma_start(xt_s[32 * q : 32 * q + 4, :].bitcast(I32), xt_scales[0, 4 * q : 4 * q + 4, :].bitcast(I32))
+        nc.scalar.dma_start(ws_stage[4:8, :].rearrange("r (q c) -> r q c", q=4), by_residue(w0_scales))
         nc.sync.dma_start(xt_w[:].bitcast(I32), xt_words[0].bitcast(I32))
-        nc.sync.dma_start(w_w[:].bitcast(I32), words_view(w_words))
+        for q in (0, 1):
+            scale_rows(nc.sync, xt_s, xt_scales, q)
         nc.sync.dma_start(xo_w[:].bitcast(I32), words_view(xo_words))
+        for q in (2, 3):
+            scale_rows(nc.sync, xt_s, xt_scales, q)
+        nc.sync.dma_start(w_w[:].bitcast(I32), words_view(w_words))
         nc.sync.dma_start(w0_w[:].bitcast(I32), words_view(w0_words))
         for q in range(4):
-            nc.scalar.dma_start(xo_s[32 * q : 32 * q + 4, :].bitcast(I32), xo_scales[0, 4 * q : 4 * q + 4, :].bitcast(I32))
-        nc.gpsimd.dma_start(ws_stage[0:4, :, :], by_residue(w_scales))
-        nc.gpsimd.dma_start(ws_stage[4:8, :, :], by_residue(w0_scales))
+            scale_rows(nc.sync if q < 3 else nc.gpsimd, xo_s, xo_scales, q)
         nc.sync.dma_start(law_lists[2][:], offs5)
         nc.sync.dma_start(sd_t[:], sd)
         nc.sync.dma_start(bd_t[:], bd)
-        nc.sync.dma_start(law_lists[3][:], offs6)
-        nc.sync.dma_start(se_t[:], se)
-        nc.sync.dma_start(be_t[:], be)
-        nc.sync.dma_start(law_lists[0][:], offs3)
-        nc.sync.dma_start(sa_t[:], sa)
-        nc.sync.dma_start(law_lists[1][:], offs4)
-        nc.sync.dma_start(sb_t[:], sb)
+        for tile, src in ((se_t, se), (be_t, be), (sa_t, sa), (sb_t, sb)):
+            nc.gpsimd.dma_start(tile[:], src)
+        for g, src in ((3, offs6), (0, offs3), (1, offs4)):
+            nc.sync.dma_start(law_lists[g][:], src)
+        nc.sync.dma_start(wbs_rows[0:4, :].rearrange("r (q c) -> r q c", q=4), by_residue(wb_scales))
         nc.sync.dma_start(wb_w[:].bitcast(I32), words_view(wb_words))
-        nc.sync.dma_start(wbs_stage[:], by_residue(wb_scales))
         nc.sync.dma_start(put_list[:], offs7)
         with nc.allow_non_contiguous_dma(reason="one float32 a partition and output tile"):
             nc.sync.dma_start(so_t[:], so.rearrange("(t p) o -> p (t o)", p=P))
 
-        nc.vector.memset(wb_s[:].bitcast(I32), 0)
         for t in range(2):
             nc.vector.memset(pages[t][:], 0.0)
 
@@ -97,15 +105,18 @@ def tile_list_quarterlaws_kernel(tc, xt_words, xt_scales, xo_words, xo_scales, w
         xt_gw = sb_tile("xt_gw", [P, J], U16)
         xo_gs = sb_tile("xo_gs", [P, J], U8)
         xo_gw = sb_tile("xo_gw", [P, J], U32)
-        nc.vector.tensor_copy(xt_gs[:], xt_s[:].indirect(tok_list[:]))
+        wd = R // 4
+        nc.vector.tensor_copy(ws_rows[32:40, 0 : 3 * wd], ws_stage[:, wd : 4 * wd])
+        nc.vector.tensor_copy(ws_rows[0:8, :].rearrange("p (h l c) -> p h l c", h=2, l=2)[:, :, 0, :],
+                              ws_stage[:, :].rearrange("p (h l c) -> p h l c", h=2, l=2)[:, :, 0, :])
+        nc.vector.tensor_copy(ws_rows[64:128, 0:wd], ws_rows[0:64, 2 * wd : 3 * wd])
+        nc.vector.tensor_copy(ws_dealt[:].rearrange("p (g q) -> p g q", g=4),
+                              ws_rows[:, 0 : R // 4].bitcast(U8).rearrange("p (q g) -> p g q", g=4))
         nc.vector.tensor_copy(xt_gw[:], xt_w[:].indirect(tok_list[:]))
-
-        for q in range(4):
-            nc.vector.tensor_copy(ws_spread[32 * q : 32 * q + 32, :].bitcast(I32), ws_stage[:, q, :])
-        nc.vector.tensor_copy(ws_dealt[:].rearrange("p (g q) -> p q g", g=4), ws_spread[:].rearrange("p (q g) -> p q g", g=4))
-
-        nc.vector.tensor_copy(xo_gs[:], xo_s[:].indirect(note_list[:]))
+        nc.vector.tensor_copy(xt_gs[:], xt_s[:].indirect(tok_list[:]))
         nc.vector.tensor_copy(xo_gw[:], xo_w[:].indirect(note_list[:]))
+        for u in range(2):
+            nc.vector.tensor_copy(xo_gs[:, u * P : (u + 1) * P], xo_s[:].indirect(note_list[:, 8 * u : 8 * u + 8]))
 
         w_d = sb_tile("w_d", [P, R], U32)
         nc.scalar.copy(w_d[:].rearrange("p (g q) -> p q g", g=4), w_w[:].rearrange("p (q g) -> p q g", g=4))
@@ -115,22 +126,33 @@ def tile_list_quarterlaws_kernel(tc, xt_words, xt_scales, xo_words, xo_scales, w
         for g0, g1 in ((2, 3), (3, 4), (0, 2)):
             nc.scalar.copy(w0_out[:, :, g0:g1], w0_in[:, :, g0:g1])
 
-        order = (2, 3, 0, 1)
-        acc = {g: psum.tile([P, J], F32, name="acc%d" % g) for g in order}
-        for g in order:
+        def token_pass(acc, g, slots, first):
             cols = slice(g * P, (g + 1) * P)
-            nc.tensor.matmul_mx(out=acc[g][:], lhsT=w_d[:, cols].bitcast(FP8X4), lhsT_scale=ws_dealt[:, cols],
-                                rhs=xt_gw[:].bitcast(FP4X4), rhs_scale=xt_gs[:], start=True, stop=False)
-        a = {}
-        for g in order:
-            cols = slice(g * P, (g + 1) * P)
-            nc.tensor.matmul_mx(out=acc[g][:], lhsT=w0_d[:, cols].bitcast(FP8X4), lhsT_scale=ws_dealt[4:P, cols],
-                                rhs=xo_gw[:].bitcast(FP8X4), rhs_scale=xo_gs[:], start=False, stop=True)
-            a[g] = sb_tile("a%d" % g, [P, J], F32)
-            nc.vector.tensor_copy(a[g][:], acc[g][:])
+            nc.tensor.matmul_mx(out=acc[:], lhsT=w_d[:, cols].bitcast(FP8X4), lhsT_scale=ws_dealt[:, cols],
+                                rhs=xt_gw[:, slots].bitcast(FP4X4), rhs_scale=xt_gs[:, slots], start=first, stop=not first)
 
-        for q in range(4):
-            nc.vector.tensor_copy(wb_s[32 * q : 32 * q + 4, :].bitcast(I32), wbs_stage[:, q, :])
+        def note_pass(acc, g, slots, first):
+            cols = slice(g * P, (g + 1) * P)
+            nc.tensor.matmul_mx(out=acc[:], lhsT=w0_d[:, cols].bitcast(FP8X4), lhsT_scale=ws_dealt[4:P, cols],
+                                rhs=xo_gw[:, slots].bitcast(FP8X4), rhs_scale=xo_gs[:, slots], start=first, stop=not first)
+
+        a = {g: sb_tile("a%d" % g, [P, J], F32) for g in range(4)}
+        halves = [slice(u * P, (u + 1) * P) for u in range(2)]
+        acc2 = [psum.tile([P, P], F32, name="bank%d" % u) for u in range(2)]
+        for u in range(2):
+            token_pass(acc2[u], 2, halves[u], True)
+        for u in range(2):
+            note_pass(acc2[u], 2, halves[u], False)
+        nc.vector.tensor_copy(a[2][:, halves[0]], acc2[0][:])
+        nc.scalar.copy(a[2][:, halves[1]], acc2[1][:])
+        for g in (3, 0, 1):
+            acc = psum.tile([P, J], F32, name="acc%d" % g)
+            note_pass(acc, g, slice(0, J), True)
+            token_pass(acc, g, slice(0, J), False)
+            nc.vector.tensor_copy(a[g][:], acc[:])
+
+        spread(wbs_rows, 4, N // 4)
+        wb_s = wbs_rows[:, 0 : N // 4].bitcast(U8)
 
         hid = sb_tile("hid", [P, 4 * O], BF16)
         nc.scalar.activation(hid[:, 2 : 4 * O : 4], a[2][:].indirect(law_lists[2][:]), ACT.Exp, bias=bd_t[:], scale=sd_t[:])
@@ -146,11 +168,14 @@ def tile_list_quarterlaws_kernel(tc, xt_words, xt_scales, xo_words, xo_scales, w
             nc.vector.quantize_mx(out=codes[:].bitcast(FP8X4), scales=scales[:], in_=hid[:, c0:c1])
             for t in range(2):
                 cols = slice(t * P, (t + 1) * P)
-                p_ps = psum.tile([P, HALF], F32, name="p_ps%d%d" % (h, t))
+                p_ps = psum.tile([P, HALF], F32, name="bank%d" % (2 * (1 - h) + t))
                 nc.tensor.matmul_mx(out=p_ps[:], lhsT=wb_w[:, cols].bitcast(FP8X4), lhsT_scale=wb_s[:, cols],
                                     rhs=codes[:].bitcast(FP8X4), rhs_scale=scales[:], start=True, stop=True)
                 p_sb[h, t] = sb_tile("p_sb%d%d" % (h, t), [P, HALF], F32)
-                nc.vector.tensor_copy(p_sb[h, t][:], p_ps[:])
+                if (h, t) == (0, 0):
+                    nc.scalar.copy(p_sb[h, t][:], p_ps[:])
+                else:
+                    nc.vector.tensor_copy(p_sb[h, t][:], p_ps[:])
         for h in range(2):
             ls = slice(h * HALF // 16, (h + 1) * HALF // 16)
             for t in range(2):

@@ -56,7 +56,6 @@ def tile_list_quarterlaws_kernel(tc, xt_words, xt_scales, xo_words, xo_scales, w
         wbs_rows = sb_tile("wbs_rows", [P, N], I32)
         ws_stage = sb_tile("ws_stage", [8, R], I32)
         ws_dealt = sb_tile("ws_dealt", [P, R], U8)
-        pages = [sb_tile("page%d" % t, [P, E], F32) for t in range(2)]
         sa_t, sb_t, sd_t, bd_t, se_t, be_t = [sb_tile(n, [P, 1], F32) for n in ("sa_t", "sb_t", "sd_t", "bd_t", "se_t", "be_t")]
         so_t = sb_tile("so_t", [P, 2], F32)
 
@@ -98,9 +97,6 @@ def tile_list_quarterlaws_kernel(tc, xt_words, xt_scales, xo_words, xo_scales, w
         with nc.allow_non_contiguous_dma(reason="one float32 a partition and output tile"):
             nc.sync.dma_start(so_t[:], so.rearrange("(t p) o -> p (t o)", p=P))
 
-        for t in range(2):
-            nc.vector.memset(pages[t][:], 0.0)
-
         xt_gs = sb_tile("xt_gs", [P, J], U8)
         xt_gw = sb_tile("xt_gw", [P, J], U16)
         xo_gs = sb_tile("xo_gs", [P, J], U8)
@@ -118,17 +114,22 @@ def tile_list_quarterlaws_kernel(tc, xt_words, xt_scales, xo_words, xo_scales, w
         for u in range(2):
             nc.vector.tensor_copy(xo_gs[:, u * P : (u + 1) * P], xo_s[:].indirect(note_list[:, 8 * u : 8 * u + 8]))
 
-        w_d = sb_tile("w_d", [P, R], U32)
-        nc.scalar.copy(w_d[:].rearrange("p (g q) -> p q g", g=4), w_w[:].rearrange("p (q g) -> p q g", g=4))
+        def deal(dealt, words, g0, g1):
+            nc.scalar.copy(dealt.rearrange("p (g q) -> p q g", g=g1 - g0),
+                           words[:].rearrange("p (q g) -> p q g", g=4)[:, :, g0:g1])
+
+        w_hi = sb_tile("w_hi", [P, 2 * P], U32)
         w0_d = sb_tile("w0_d", [P, R], U32)
-        w0_in = w0_w[:].rearrange("p (q g) -> p q g", g=4)
-        w0_out = w0_d[:].rearrange("p (g q) -> p q g", g=4)
+        for g in (2, 3):
+            deal(w_hi[:, (g - 2) * P : (g - 1) * P], w_w, g, g + 1)
         for g0, g1 in ((2, 3), (3, 4), (0, 2)):
-            nc.scalar.copy(w0_out[:, :, g0:g1], w0_in[:, :, g0:g1])
+            deal(w0_d[:, g0 * P : g1 * P], w0_w, g0, g1)
+        w_lo = keep.tile([P, 2 * P], U32, name="w_lo", tag="w0_w", align_bytes=64)
+        deal(w_lo[:], w_w, 0, 2)
 
         def token_pass(acc, g, slots, first):
             cols = slice(g * P, (g + 1) * P)
-            nc.tensor.matmul_mx(out=acc[:], lhsT=w_d[:, cols].bitcast(FP8X4), lhsT_scale=ws_dealt[:, cols],
+            nc.tensor.matmul_mx(out=acc[:], lhsT=(w_lo, w_hi)[g // 2][:, (g % 2) * P : (g % 2 + 1) * P].bitcast(FP8X4), lhsT_scale=ws_dealt[:, cols],
                                 rhs=xt_gw[:, slots].bitcast(FP4X4), rhs_scale=xt_gs[:, slots], start=first, stop=not first)
 
         def note_pass(acc, g, slots, first):
@@ -152,6 +153,9 @@ def tile_list_quarterlaws_kernel(tc, xt_words, xt_scales, xo_words, xo_scales, w
             nc.vector.tensor_copy(a[g][:], acc[:])
 
         spread(wbs_rows, 4, N // 4)
+        pages = [keep.tile([P, E], F32, name="page%d" % t, tag=("w_hi", "w0_d")[t], align_bytes=64) for t in range(2)]
+        for t in range(2):
+            nc.vector.memset(pages[t][:], 0.0)
         wb_s = wbs_rows[:, 0 : N // 4].bitcast(U8)
 
         hid = sb_tile("hid", [P, 4 * O], BF16)

from contextlib import ExitStack

import concourse.mybir as mybir

K, T, J, R, O, N, E = 512, 1024, 256, 512, 128, 256, 256
FLOPS = 2 * (2 * K * R * J + R * N * O)

F32 = mybir.dt.float32
BF16 = mybir.dt.bfloat16
I32 = mybir.dt.int32
U32 = mybir.dt.uint32
U16 = mybir.dt.uint16
U8 = mybir.dt.uint8
FP8X4 = mybir.dt.float8_e4m3fn_x4
FP4X4 = mybir.dt.float4_e2m1fn_x4
ACT = mybir.ActivationFunctionType

P = 128
HALF = O // 2


def tile_list_quarterlaws_kernel(tc, xt_words, xt_scales, xo_words, xo_scales, w_words, w_scales,
                                      w0_words, w0_scales, sa, sb, sd, bd, se, be, wb_words, wb_scales, so,
                                      offs, offs2, offs3, offs4, offs5, offs6, offs7, out):
    nc = tc.nc
    with ExitStack() as ctx:
        keep = ctx.enter_context(tc.tile_pool(name="keep", bufs=1))
        psum = ctx.enter_context(tc.psum_pool(name="psum", bufs=1))

        def sb_tile(name, shape, dtype):
            return keep.tile(shape, dtype, name=name, align_bytes=64)

        def words_view(words):
            return words[0].rearrange("p n t -> p (n t)").bitcast(I32)

        def by_residue(scales):
            return scales[0].bitcast(I32).rearrange("(q r) c -> r q c", r=4)

        def spread(rows, live, width):
            nc.vector.tensor_copy(rows[32 : 32 + live, 0 : 3 * width], rows[0:live, width : 4 * width])
            nc.vector.tensor_copy(rows[64:128, 0:width], rows[0:64, 2 * width : 3 * width])

        tok_list = sb_tile("tok_list", [P, J // 16], U16)
        note_list = sb_tile("note_list", [P, J // 16], U16)
        law_lists = [sb_tile("law_list%d" % g, [P, O // 16], U16) for g in range(4)]
        put_list = sb_tile("put_list", [P, O // 16], U16)

        xt_w = sb_tile("xt_w", [P, T], U16)
        xt_s = sb_tile("xt_s", [P, T], U8)
        xo_w = sb_tile("xo_w", [P, T], U32)
        xo_s = sb_tile("xo_s", [P, T], U8)
        w_w = sb_tile("w_w", [P, R], U32)
        w0_w = sb_tile("w0_w", [P, R], U32)
        wb_w = sb_tile("wb_w", [P, N], U32)
        ws_rows = sb_tile("ws_rows", [P, R], I32)
        wbs_rows = sb_tile("wbs_rows", [P, N], I32)
        ws_stage = sb_tile("ws_stage", [8, R], I32)
        ws_dealt = sb_tile("ws_dealt", [P, R], U8)
        sa_t, sb_t, sd_t, bd_t, se_t, be_t = [sb_tile(n, [P, 1], F32) for n in ("sa_t", "sb_t", "sd_t", "bd_t", "se_t", "be_t")]
        so_t = sb_tile("so_t", [P, 2], F32)

        def clear_even_blocks(engine, rows):
            engine.memset(rows[0:64, :].rearrange("p (h l c) -> p h l c", h=2, l=2)[:, :, 0, :], 0)

        nc.vector.memset(xo_s[:].bitcast(I32), 0)
        nc.vector.memset(xt_s[:].bitcast(I32), 0)
        clear_even_blocks(nc.vector, ws_rows)
        clear_even_blocks(nc.vector, wbs_rows)

        def scale_rows(queue, plane, scales, q):
            queue.dma_start(plane[32 * q : 32 * q + 4, :].bitcast(I32), scales[0, 4 * q : 4 * q + 4, :].bitcast(I32))

        nc.sync.dma_start(tok_list[:], offs)
        nc.scalar.dma_start(ws_stage[0:4, :].rearrange("r (q c) -> r q c", q=4), by_residue(w_scales))
        nc.sync.dma_start(note_list[:], offs2)
        nc.scalar.dma_start(ws_stage[4:8, :].rearrange("r (q c) -> r q c", q=4), by_residue(w0_scales))
        nc.sync.dma_start(xt_w[:].bitcast(I32), xt_words[0].bitcast(I32))
        for q in (0, 1):
            scale_rows(nc.sync, xt_s, xt_scales, q)
        nc.sync.dma_start(xo_w[:].bitcast(I32), words_view(xo_words))
        for q in (2, 3):
            scale_rows(nc.sync, xt_s, xt_scales, q)
        nc.sync.dma_start(w_w[:].bitcast(I32), words_view(w_words))
        nc.sync.dma_start(w0_w[:].bitcast(I32), words_view(w0_words))
        for q in range(4):
            scale_rows(nc.sync if q < 3 else nc.gpsimd, xo_s, xo_scales, q)
        nc.sync.dma_start(law_lists[2][:], offs5)
        nc.sync.dma_start(sd_t[:], sd)
        nc.sync.dma_start(bd_t[:], bd)
        for tile, src in ((se_t, se), (be_t, be), (sa_t, sa), (sb_t, sb)):
            nc.gpsimd.dma_start(tile[:], src)
        for g, src in ((3, offs6), (0, offs3), (1, offs4)):
            nc.sync.dma_start(law_lists[g][:], src)
        nc.sync.dma_start(wbs_rows[0:4, :].rearrange("r (q c) -> r q c", q=4), by_residue(wb_scales))
        nc.sync.dma_start(wb_w[:].bitcast(I32), words_view(wb_words))
        nc.sync.dma_start(put_list[:], offs7)
        with nc.allow_non_contiguous_dma(reason="one float32 a partition and output tile"):
            nc.sync.dma_start(so_t[:], so.rearrange("(t p) o -> p (t o)", p=P))

        xt_gs = sb_tile("xt_gs", [P, J], U8)
        xt_gw = sb_tile("xt_gw", [P, J], U16)
        xo_gs = sb_tile("xo_gs", [P, J], U8)
        xo_gw = sb_tile("xo_gw", [P, J], U32)
        wd = R // 4
        nc.vector.tensor_copy(ws_rows[32:40, 0 : 3 * wd], ws_stage[:, wd : 4 * wd])
        nc.vector.tensor_copy(ws_rows[0:8, :].rearrange("p (h l c) -> p h l c", h=2, l=2)[:, :, 0, :],
                              ws_stage[:, :].rearrange("p (h l c) -> p h l c", h=2, l=2)[:, :, 0, :])
        nc.vector.tensor_copy(ws_rows[64:128, 0:wd], ws_rows[0:64, 2 * wd : 3 * wd])
        nc.vector.tensor_copy(ws_dealt[:].rearrange("p (g q) -> p g q", g=4),
                              ws_rows[:, 0 : R // 4].bitcast(U8).rearrange("p (q g) -> p g q", g=4))
        nc.vector.tensor_copy(xt_gw[:], xt_w[:].indirect(tok_list[:]))
        nc.vector.tensor_copy(xt_gs[:], xt_s[:].indirect(tok_list[:]))
        nc.vector.tensor_copy(xo_gw[:], xo_w[:].indirect(note_list[:]))
        for u in range(2):
            nc.vector.tensor_copy(xo_gs[:, u * P : (u + 1) * P], xo_s[:].indirect(note_list[:, 8 * u : 8 * u + 8]))

        def deal(dealt, words, g0, g1):
            nc.scalar.copy(dealt.rearrange("p (g q) -> p q g", g=g1 - g0),
                           words[:].rearrange("p (q g) -> p q g", g=4)[:, :, g0:g1])

        w_hi = sb_tile("w_hi", [P, 2 * P], U32)
        w0_d = sb_tile("w0_d", [P, R], U32)
        for g in (2, 3):
            deal(w_hi[:, (g - 2) * P : (g - 1) * P], w_w, g, g + 1)
        for g0, g1 in ((2, 3), (3, 4), (0, 2)):
            deal(w0_d[:, g0 * P : g1 * P], w0_w, g0, g1)
        w_lo = keep.tile([P, 2 * P], U32, name="w_lo", tag="w0_w", align_bytes=64)
        deal(w_lo[:], w_w, 0, 2)

        def token_pass(acc, g, slots, first):
            cols = slice(g * P, (g + 1) * P)
            nc.tensor.matmul_mx(out=acc[:], lhsT=(w_lo, w_hi)[g // 2][:, (g % 2) * P : (g % 2 + 1) * P].bitcast(FP8X4), lhsT_scale=ws_dealt[:, cols],
                                rhs=xt_gw[:, slots].bitcast(FP4X4), rhs_scale=xt_gs[:, slots], start=first, stop=not first)

        def note_pass(acc, g, slots, first):
            cols = slice(g * P, (g + 1) * P)
            nc.tensor.matmul_mx(out=acc[:], lhsT=w0_d[:, cols].bitcast(FP8X4), lhsT_scale=ws_dealt[4:P, cols],
                                rhs=xo_gw[:, slots].bitcast(FP8X4), rhs_scale=xo_gs[:, slots], start=first, stop=not first)

        a = {g: sb_tile("a%d" % g, [P, J], F32) for g in range(4)}
        halves = [slice(u * P, (u + 1) * P) for u in range(2)]
        acc2 = [psum.tile([P, P], F32, name="bank%d" % u) for u in range(2)]
        for u in range(2):
            token_pass(acc2[u], 2, halves[u], True)
        for u in range(2):
            note_pass(acc2[u], 2, halves[u], False)
        nc.vector.tensor_copy(a[2][:, halves[0]], acc2[0][:])
        nc.scalar.copy(a[2][:, halves[1]], acc2[1][:])
        for g in (3, 0, 1):
            acc = psum.tile([P, J], F32, name="acc%d" % g)
            note_pass(acc, g, slice(0, J), True)
            token_pass(acc, g, slice(0, J), False)
            nc.vector.tensor_copy(a[g][:], acc[:])

        spread(wbs_rows, 4, N // 4)
        pages = [keep.tile([P, E], F32, name="page%d" % t, tag=("w_hi", "w0_d")[t], align_bytes=64) for t in range(2)]
        for t in range(2):
            nc.vector.memset(pages[t][:], 0.0)
        wb_s = wbs_rows[:, 0 : N // 4].bitcast(U8)

        hid = sb_tile("hid", [P, 4 * O], BF16)
        nc.scalar.activation(hid[:, 2 : 4 * O : 4], a[2][:].indirect(law_lists[2][:]), ACT.Exp, bias=bd_t[:], scale=sd_t[:])
        p_sb = {}
        for h in range(2):
            c0, c1 = 4 * HALF * h, 4 * HALF * (h + 1)
            ls = slice(h * HALF // 16, (h + 1) * HALF // 16)
            nc.scalar.activation(hid[:, c0 + 3 : c1 : 4], a[3][:].indirect(law_lists[3][:, ls]), ACT.Sigmoid, bias=be_t[:], scale=se_t[:])
            nc.scalar.activation(hid[:, c0 : c1 : 4], a[0][:].indirect(law_lists[0][:, ls]), ACT.Copy, scale=sa_t[:])
            nc.scalar.activation(hid[:, c0 + 1 : c1 : 4], a[1][:].indirect(law_lists[1][:, ls]), ACT.Copy, scale=sb_t[:])
            codes = sb_tile("codes%d" % h, [P, HALF], U32)
            scales = sb_tile("scales%d" % h, [P, HALF], U8)
            nc.vector.quantize_mx(out=codes[:].bitcast(FP8X4), scales=scales[:], in_=hid[:, c0:c1])
            for t in range(2):
                cols = slice(t * P, (t + 1) * P)
                p_ps = psum.tile([P, HALF], F32, name="bank%d" % (2 * (1 - h) + t))
                nc.tensor.matmul_mx(out=p_ps[:], lhsT=wb_w[:, cols].bitcast(FP8X4), lhsT_scale=wb_s[:, cols],
                                    rhs=codes[:].bitcast(FP8X4), rhs_scale=scales[:], start=True, stop=True)
                p_sb[h, t] = sb_tile("p_sb%d%d" % (h, t), [P, HALF], F32)
                if (h, t) == (0, 0):
                    nc.scalar.copy(p_sb[h, t][:], p_ps[:])
                else:
                    nc.vector.tensor_copy(p_sb[h, t][:], p_ps[:])
        for h in range(2):
            ls = slice(h * HALF // 16, (h + 1) * HALF // 16)
            for t in range(2):
                nc.scalar.activation(pages[t][:].indirect(put_list[:, ls]), p_sb[h, t][:], ACT.Copy, scale=so_t[:, t : t + 1])
        for t in range(2):
            nc.sync.dma_start(out[t * P : (t + 1) * P, :], pages[t][:])
